import numpy as np
import ml_dtypes


def mxq(x, axis, fmt="e4m3"):
    dtype, down = {"e4m3": (ml_dtypes.float8_e4m3fn, 7), "e5m2": (ml_dtypes.float8_e5m2, 14)}[fmt]
    v = np.moveaxis(np.asarray(x, np.float32).astype(ml_dtypes.bfloat16).astype(np.float64), axis, -1)
    blocks = v.reshape(v.shape[:-1] + (-1, 32))
    amax = np.abs(blocks).max(-1, keepdims=True)
    byte = np.maximum(np.where(amax > 0, np.frexp(amax)[1] - 1 + 127, 0) - down, 1)
    scale = np.exp2(byte - 127.0)
    codes = (blocks / scale).astype(np.float32).astype(dtype).astype(np.float64)
    return np.moveaxis((codes * scale).reshape(v.shape), -1, axis)


WIDE = False


def mx_kscale(k):
    if not WIDE:
        return np.ones(k)
    levels = np.array([24, -24, 12, -12, 0])
    if k % 512:
        return np.exp2(np.random.permutation(np.resize(levels, k // 32))).repeat(32)
    a = np.empty((k // 512, 16))
    for p in range(k // 512):
        a[p, :8] = np.random.permutation(np.resize(levels, 8))
        for g in range(8):
            far = levels[np.abs(levels - a[p, g]) >= 10]
            a[p, g + 8] = far[np.random.randint(len(far))]
    return np.exp2(a.ravel()).repeat(32)


def f64(x):
    return np.asarray(x).astype(np.float64)


E2M1 = np.array([0.0, 0.5, 1.0, 1.5, 2.0, 3.0, 4.0, 6.0, -0.0, -0.5, -1.0, -1.5, -2.0, -3.0, -4.0, -6.0])


def pack_weight(w, fmt):
    k, n = w.shape
    w = f64(np.asarray(w, np.float32).astype(ml_dtypes.bfloat16)).reshape(k // 32, 32, n)
    amax = np.abs(w).max(1)
    if fmt == "e4m3":
        byte = np.frexp(amax)[1] - 1 + 127 - 7
    else:
        mant, ex = np.frexp(amax / 6.0)
        byte = np.where(mant > 0.5, ex, ex - 1) + 127
    byte = np.clip(np.where(amax > 0, byte, 1), 1, 254)
    scaled = (w * np.exp2(127.0 - byte)[:, None, :]).reshape(k, n).astype(np.float32)
    by_word = np.ascontiguousarray(scaled.reshape(k // 512, 128, 4, n).transpose(0, 1, 3, 2))
    if fmt == "e4m3":
        words = by_word.astype(ml_dtypes.float8_e4m3fn).view(np.uint8)
    else:
        c = by_word.astype(ml_dtypes.float4_e2m1fn).view(np.uint8) & 0xF
        words = (c[..., 0::2] | (c[..., 1::2] << 4)).reshape(k // 512, 128, 2 * n)
    return np.ascontiguousarray(words), np.ascontiguousarray(byte.astype(np.uint8).reshape(k // 512, 16, n))


def unpack_weight(words, scales, fmt):
    g, _, n = scales.shape
    words = np.ascontiguousarray(words).reshape(g, 128, n, -1)
    if fmt == "e4m3":
        vals = words.view(ml_dtypes.float8_e4m3fn).astype(np.float64)
    else:
        nib = np.empty((g, 128, n, 4), np.uint8)
        nib[..., 0::2] = words & 0xF
        nib[..., 1::2] = words >> 4
        vals = E2M1[nib]
    vals = vals * np.repeat(np.exp2(scales.astype(np.float64) - 127.0), 8, axis=1)[..., None]
    return vals.transpose(0, 1, 3, 2).reshape(g * 512, n)


K, N, T = 512, 512, 512


def setup_inputs():
    n = np.random.standard_normal
    s = mx_kscale(K)[:, None]
    p_wr = pack_weight(n((K, N)) / np.sqrt(4 * K) / s, "e4m3")
    p_wi = pack_weight(n((K, N)) / np.sqrt(4 * K) / s, "e2m1")
    p_wj = pack_weight(n((K, N)) / np.sqrt(4 * K) / s, "e2m1")
    p_wk = pack_weight(n((K, N)) / np.sqrt(4 * K) / s, "e2m1")
    return {
        "xr": (n((K, T)) * s).astype(np.float32),
        "xi": (n((K, T)) * s).astype(np.float32),
        "xj": (n((K, T)) * s).astype(np.float32),
        "xk": (n((K, T)) * s).astype(np.float32),
        "wr_words": p_wr[0],
        "wr_scales": p_wr[1],
        "wi_words": p_wi[0],
        "wi_scales": p_wi[1],
        "wj_words": p_wj[0],
        "wj_scales": p_wj[1],
        "wk_words": p_wk[0],
        "wk_scales": p_wk[1],
    }


def reference(xr, xi, xj, xk, wr_words, wr_scales, wi_words, wi_scales, wj_words, wj_scales, wk_words, wk_scales):
    xr_ = mxq(f64(xr), 0, "e4m3")
    xi_ = mxq(f64(xi), 0, "e4m3")
    xj_ = mxq(f64(xj), 0, "e4m3")
    xk_ = mxq(f64(xk), 0, "e4m3")
    wr_ = unpack_weight(wr_words, wr_scales, "e4m3")
    wi_ = unpack_weight(wi_words, wi_scales, "e2m1")
    wj_ = unpack_weight(wj_words, wj_scales, "e2m1")
    wk_ = unpack_weight(wk_words, wk_scales, "e2m1")
    pr = wr_.T @ xr_
    mr = wi_.T @ xi_ + wj_.T @ xj_ + wk_.T @ xk_
    pi = wr_.T @ xi_ + wi_.T @ xr_ + wj_.T @ xk_
    mi = wk_.T @ xj_
    pj = wr_.T @ xj_ + wj_.T @ xr_ + wk_.T @ xi_
    mj = wi_.T @ xk_
    pk = wr_.T @ xk_ + wi_.T @ xj_ + wk_.T @ xr_
    mk = wj_.T @ xi_
    return np.maximum(pr - mr, 0.0), np.maximum(pi - mi, 0.0), np.maximum(pj - mj, 0.0), np.maximum(pk - mk, 0.0)

@@ -1,0 +1,189 @@
+from contextlib import ExitStack
+
+import concourse.mybir as mybir
+
+K, N, T = 512, 512, 512
+FLOPS = 16 * 2 * K * N * T
+
+F32 = mybir.dt.float32
+BF16 = mybir.dt.bfloat16
+I32 = mybir.dt.int32
+U32 = mybir.dt.uint32
+U8 = mybir.dt.uint8
+FP8X4 = mybir.dt.float8_e4m3fn_x4
+FP4X4 = mybir.dt.float4_e2m1fn_x4
+ACT = mybir.ActivationFunctionType
+ALU = mybir.AluOpType
+
+P = 128
+PACK = 4
+HALF = T // 2
+QUARTER = T // 4
+TILES = N // P
+BANKS = 8
+F32_MAX = 3.4028234663852886e38
+
+
+def tile_mix_quat_relu_kernel(
+    tc, xr, xi, xj, xk,
+    wr_words, wr_scales, wi_words, wi_scales, wj_words, wj_scales, wk_words, wk_scales,
+    out_0, out_1, out_2, out_3,
+):
+    nc = tc.nc
+    x_hbm = {"r": xr, "i": xi, "j": xj, "k": xk}
+    words_hbm = {
+        "r": wr_words[0].rearrange("p n t -> p (n t)"),
+        "i": wi_words[0],
+        "j": wj_words[0],
+        "k": wk_words[0],
+    }
+    scales_hbm = {"r": wr_scales[0], "i": wi_scales[0], "j": wj_scales[0], "k": wk_scales[0]}
+    out_hbm = {"r": out_0, "i": out_1, "j": out_2, "k": out_3}
+    word_size = {"r": 4, "i": 2, "j": 2, "k": 2}
+    word_view = {"r": FP8X4, "i": FP4X4, "j": FP4X4, "k": FP4X4}
+
+    with ExitStack() as ctx:
+        keep = ctx.enter_context(tc.tile_pool(name="keep", bufs=1))
+        psum = ctx.enter_context(tc.psum_pool(name="psum", bufs=1))
+        ctx.enter_context(tc.manual_schedule())
+
+        w_words, w_scales, x_raw, x_codes, x_scales, minus = {}, {}, {}, {}, {}, {}
+        for c in "jikr":
+            w_words[c] = keep.tile([P, N * word_size[c]], U8, name="w_words_" + c, align_bytes=64)
+            w_scales[c] = keep.tile([P, N], U8, name="w_scales_" + c, align_bytes=64)
+            x_codes[c] = keep.tile([P, T], U32, name="x_codes_" + c, align_bytes=64)
+            x_scales[c] = keep.tile([P, T], U8, name="x_scales_" + c, align_bytes=64)
+            nc.vector.memset(w_scales[c][:].bitcast(U32), 0)
+
+        def load_x(c, h):
+            x_raw[c, h] = keep.tile([P, PACK, HALF], F32, name="x_raw_%s%d" % (c, h), align_bytes=64)
+            rows = x_hbm[c].rearrange("(p j) t -> p j t", j=PACK)
+            nc.sync.dma_start(out=x_raw[c, h][:], in_=rows[:, :, h * HALF : (h + 1) * HALF])
+
+        def load_words(c):
+            nc.sync.dma_start(out=w_words[c][:].bitcast(I32), in_=words_hbm[c].bitcast(I32))
+
+        def load_scales(c):
+            for r in range(4):
+                nc.sync.dma_start(
+                    out=w_scales[c][r:P:32, :].bitcast(I32), in_=scales_hbm[c][r:16:4, :].bitcast(I32)
+                )
+
+        load_x("i", 0)
+        load_words("j")
+        load_scales("j")
+        load_x("i", 1)
+        load_words("i")
+        load_scales("i")
+        load_x("j", 0)
+        load_words("k")
+        load_scales("k")
+        load_x("j", 1)
+        load_x("k", 0)
+        load_x("k", 1)
+        load_scales("r")
+        load_x("r", 0)
+        load_x("r", 1)
+        load_words("r")
+
+        def quantize_half(c, h):
+            grouped = []
+            for q in range(2):
+                g = keep.tile([P, QUARTER, PACK], BF16, name="grouped_%s%d%d" % (c, h, q), align_bytes=64)
+                nc.vector.tensor_copy(
+                    out=g[:].rearrange("p (c i) t -> p c t i", i=4),
+                    in_=x_raw[c, h][:, :, q * QUARTER : (q + 1) * QUARTER].rearrange("p t (c i) -> p c t i", i=4),
+                )
+                grouped.append(g)
+            for q in range(2):
+                cols = slice(h * HALF + q * QUARTER, h * HALF + (q + 1) * QUARTER)
+                nc.vector.quantize_mx(
+                    out=x_codes[c][:, cols].bitcast(FP8X4),
+                    scales=x_scales[c][:, cols],
+                    in_=grouped[q][:].rearrange("p w t -> p (w t)"),
+                )
+
+        def bank(b):
+            return psum.tile([P, T], F32, name="bank%d" % b)
+
+        def product(acc, w, x, a, cols, start, stop):
+            nc.tensor.matmul_mx(
+                out=acc,
+                lhsT=w_words[w][:, a * P * word_size[w] : (a + 1) * P * word_size[w]].bitcast(word_view[w]),
+                lhsT_scale=w_scales[w][:, a * P : (a + 1) * P],
+                rhs=x_codes[x][:, cols].bitcast(FP8X4),
+                rhs_scale=x_scales[x][:, cols],
+                start=start,
+                stop=stop,
+            )
+
+        for c in "rijk":
+            minus[c] = keep.tile([P, TILES, T], F32, name="minus_" + c)
+
+        whole = slice(0, T)
+        halves = [slice(0, HALF), slice(HALF, T)]
+
+        m_r = [bank(TILES + a) for a in range(TILES)]
+        for x, lone_out, lone_w in (("i", "k", "j"), ("j", "i", "k"), ("k", "j", "i")):
+            for h in range(2):
+                quantize_half(x, h)
+                for u in range(2):
+                    lone = bank(2 * h + u)
+                    for v in range(2):
+                        product(lone[:, halves[v]], lone_w, x, 2 * u + v, halves[h], True, True)
+                    nc.scalar.activation(
+                        out=minus[lone_out][:, 2 * u : 2 * u + 2, halves[h]],
+                        in_=lone[:].rearrange("p (v t) -> p v t", v=2),
+                        func=ACT.Copy,
+                    )
+            for a in range(TILES):
+                product(m_r[a][:], x, x, a, whole, x == "i", x == "k")
+        for a in range(TILES):
+            nc.scalar.activation(out=minus["r"][:, a, :], in_=m_r[a][:], func=ACT.Copy)
+        quantize_half("r", 0)
+        quantize_half("r", 1)
+
+        plus = {
+            "r": [("r", "r")],
+            "i": [("j", "k"), ("i", "r"), ("r", "i")],
+            "j": [("k", "i"), ("j", "r"), ("r", "j")],
+            "k": [("i", "j"), ("k", "r"), ("r", "k")],
+        }
+
+        def relu(engine, res, diff):
+            if engine == "scalar":
+                nc.scalar.activation(out=res, in_=diff, func=ACT.Relu)
+            elif engine == "vector":
+                nc.vector.tensor_scalar_max(out=res, in0=diff, scalar1=0.0)
+            else:
+                nc.gpsimd.tensor_scalar(out=res, in0=diff, scalar1=F32_MAX, scalar2=0.0, op0=ALU.min, op1=ALU.max)
+
+        def finish(c, a, acc, pieces):
+            diffs = []
+            for n, (cols, engine) in enumerate(pieces):
+                diff = keep.tile([P, cols.stop - cols.start], F32, name="diff_%s%d%d" % (c, a, n))
+                nc.vector.tensor_tensor(out=diff[:], in0=acc[:, cols], in1=minus[c][:, a, cols], op=ALU.subtract)
+                diffs.append(diff)
+            for n, (cols, engine) in enumerate(pieces):
+                res = keep.tile([P, cols.stop - cols.start], F32, name="res_%s%d%d" % (c, a, n))
+                relu(engine, res[:], diffs[n][:])
+                nc.sync.dma_start(out=out_hbm[c][a * P : (a + 1) * P, cols], in_=res[:])
+
+        acc = {c: bank(b) for b, c in enumerate("ijk")}
+        for c in "ijk":
+            product(acc[c][:], *plus[c][0], 0, whole, True, False)
+        for c in "ijk":
+            product(acc[c][:], *plus[c][1], 0, whole, False, False)
+            product(acc[c][:], *plus[c][2], 0, whole, False, True)
+            finish(c, 0, acc[c], [(whole, "gpsimd")])
+        group = 3
+        for a in range(TILES):
+            for c in "r" if a == 0 else "rijk":
+                sums = bank(group % BANKS)
+                for s, (w, x) in enumerate(plus[c]):
+                    product(sums[:], w, x, a, whole, s == 0, s == len(plus[c]) - 1)
+                if group == 4 * TILES - 1:
+                    finish(c, a, sums, [(halves[0], "scalar"), (halves[1], "vector")])
+                else:
+                    finish(c, a, sums, [(whole, "scalar")])
+                group = group + 1

@@ -21,6 +21,7 @@ HALF = T // 2
 QUARTER = T // 4
 TILES = N // P
 BANKS = 8
+WARM_PASSES = 0
 F32_MAX = 3.4028234663852886e38
 
 
@@ -53,6 +54,8 @@ def tile_mix_quat_relu_kernel(
             w_scales[c] = keep.tile([P, N], U8, name="w_scales_" + c, align_bytes=64)
             x_codes[c] = keep.tile([P, T], U32, name="x_codes_" + c, align_bytes=64)
             x_scales[c] = keep.tile([P, T], U8, name="x_scales_" + c, align_bytes=64)
+            minus[c] = keep.tile([P, TILES, T], F32, name="minus_" + c)
+        for c in "jikr":
             nc.vector.memset(w_scales[c][:].bitcast(U32), 0)
 
         def load_x(c, h):
@@ -73,17 +76,17 @@ def tile_mix_quat_relu_kernel(
         load_words("j")
         load_scales("j")
         load_x("i", 1)
+        load_x("k", 0)
         load_words("i")
         load_scales("i")
+        load_x("k", 1)
         load_x("j", 0)
         load_words("k")
         load_scales("k")
         load_x("j", 1)
-        load_x("k", 0)
-        load_x("k", 1)
-        load_scales("r")
         load_x("r", 0)
         load_x("r", 1)
+        load_scales("r")
         load_words("r")
 
         def quantize_half(c, h):
@@ -117,32 +120,8 @@ def tile_mix_quat_relu_kernel(
                 stop=stop,
             )
 
-        for c in "rijk":
-            minus[c] = keep.tile([P, TILES, T], F32, name="minus_" + c)
-
         whole = slice(0, T)
         halves = [slice(0, HALF), slice(HALF, T)]
-
-        m_r = [bank(TILES + a) for a in range(TILES)]
-        for x, lone_out, lone_w in (("i", "k", "j"), ("j", "i", "k"), ("k", "j", "i")):
-            for h in range(2):
-                quantize_half(x, h)
-                for u in range(2):
-                    lone = bank(2 * h + u)
-                    for v in range(2):
-                        product(lone[:, halves[v]], lone_w, x, 2 * u + v, halves[h], True, True)
-                    nc.scalar.activation(
-                        out=minus[lone_out][:, 2 * u : 2 * u + 2, halves[h]],
-                        in_=lone[:].rearrange("p (v t) -> p v t", v=2),
-                        func=ACT.Copy,
-                    )
-            for a in range(TILES):
-                product(m_r[a][:], x, x, a, whole, x == "i", x == "k")
-        for a in range(TILES):
-            nc.scalar.activation(out=minus["r"][:, a, :], in_=m_r[a][:], func=ACT.Copy)
-        quantize_half("r", 0)
-        quantize_half("r", 1)
-
         plus = {
             "r": [("r", "r")],
             "i": [("j", "k"), ("i", "r"), ("r", "i")],
@@ -150,6 +129,52 @@ def tile_mix_quat_relu_kernel(
             "k": [("i", "j"), ("k", "r"), ("r", "k")],
         }
 
+        def lone_sum(c, w, x, h, b):
+            lone = bank(b)
+            u = b % 2
+            for v in range(2):
+                product(lone[:, halves[v]], w, x, 2 * u + v, halves[h], True, True)
+            nc.scalar.activation(
+                out=minus[c][:, 2 * u : 2 * u + 2, halves[h]],
+                in_=lone[:].rearrange("p (v t) -> p v t", v=2),
+                func=ACT.Copy,
+            )
+
+        def mr_half(x, h, tiles):
+            for a in tiles:
+                for q in range(2):
+                    part = slice(h * HALF + q * QUARTER, h * HALF + (q + 1) * QUARTER)
+                    product(m_r[a][:, part], x, x, a, part, False, h == 1 and q == 1)
+
+        m_r = [bank(TILES + a) for a in range(TILES)]
+        opened = {}
+
+        def open_sum(c, a, b):
+            opened[c, a] = (bank(b), b)
+            product(opened[c, a][0][:], *plus[c][0], a, whole, True, c == "r")
+
+        for x, lone_out, lone_w in (("i", "k", "j"), ("k", "j", "i"), ("j", "i", "k")):
+            quantize_half(x, 0)
+            lone_sum(lone_out, lone_w, x, 0, 0)
+            lone_sum(lone_out, lone_w, x, 0, 1)
+            quantize_half(x, 1)
+            if x != "j":
+                lone_sum(lone_out, lone_w, x, 1, 2)
+                lone_sum(lone_out, lone_w, x, 1, 3)
+                for a in range(TILES):
+                    product(m_r[a][:], x, x, a, whole, x == "i", False)
+        open_sum("j", 0, 2)
+        open_sum("i", 0, 3)
+        for step in (0, 4, 1, 2, 5, 3):
+            if step >= TILES:
+                lone_sum("i", "k", "j", 1, step - TILES)
+            else:
+                product(m_r[step][:], "j", "j", step, whole, False, True)
+        for a in range(TILES):
+            nc.scalar.activation(out=minus["r"][:, a, :], in_=m_r[a][:], func=ACT.Copy)
+        quantize_half("r", 0)
+        quantize_half("r", 1)
+        open_sum("k", 0, 0)
         def relu(engine, res, diff):
             if engine == "scalar":
                 nc.scalar.activation(out=res, in_=diff, func=ACT.Relu)
@@ -160,30 +185,35 @@ def tile_mix_quat_relu_kernel(
 
         def finish(c, a, acc, pieces):
             diffs = []
-            for n, (cols, engine) in enumerate(pieces):
-                diff = keep.tile([P, cols.stop - cols.start], F32, name="diff_%s%d%d" % (c, a, n))
+            for cols, engine in pieces:
+                diff = keep.tile([P, cols.stop - cols.start], F32, name="diff_%s%d_%d" % (c, a, cols.start))
                 nc.vector.tensor_tensor(out=diff[:], in0=acc[:, cols], in1=minus[c][:, a, cols], op=ALU.subtract)
                 diffs.append(diff)
-            for n, (cols, engine) in enumerate(pieces):
-                res = keep.tile([P, cols.stop - cols.start], F32, name="res_%s%d%d" % (c, a, n))
-                relu(engine, res[:], diffs[n][:])
+            for diff, (cols, engine) in zip(diffs, pieces):
+                res = keep.tile([P, cols.stop - cols.start], F32, name="res_%s%d_%d" % (c, a, cols.start))
+                relu(engine, res[:], diff[:])
                 nc.sync.dma_start(out=out_hbm[c][a * P : (a + 1) * P, cols], in_=res[:])
 
-        acc = {c: bank(b) for b, c in enumerate("ijk")}
-        for c in "ijk":
-            product(acc[c][:], *plus[c][0], 0, whole, True, False)
-        for c in "ijk":
-            product(acc[c][:], *plus[c][1], 0, whole, False, False)
-            product(acc[c][:], *plus[c][2], 0, whole, False, True)
-            finish(c, 0, acc[c], [(whole, "gpsimd")])
-        group = 3
-        for a in range(TILES):
-            for c in "r" if a == 0 else "rijk":
-                sums = bank(group % BANKS)
-                for s, (w, x) in enumerate(plus[c]):
-                    product(sums[:], w, x, a, whole, s == 0, s == len(plus[c]) - 1)
-                if group == 4 * TILES - 1:
-                    finish(c, a, sums, [(halves[0], "scalar"), (halves[1], "vector")])
-                else:
-                    finish(c, a, sums, [(whole, "scalar")])
-                group = group + 1
+        free = [1, 4, 5, 6, 7]
+        order = [(c, 0) for c in "jikr"] + [(c, a) for a in (1, 2, 3) for c in "rijk"]
+        for n, (c, a) in enumerate(order[:-1]):
+            if (c, a) not in opened:
+                open_sum(c, a, free.pop(0))
+            sums, b = opened[c, a]
+            for s, (w, x) in enumerate(plus[c][1:]):
+                product(sums[:], w, x, a, whole, False, s == 1)
+            if n >= len(order) - 2:
+                finish(c, a, sums, [(halves[0], "scalar"), (halves[1], "scalar")])
+            else:
+                finish(c, a, sums, [(whole, "gpsimd" if n < 2 else "scalar")])
+            free.append(b)
+        c, a = order[-1]
+        for cols, engine in ((halves[0], "scalar"), (halves[1], "vector")):
+            sums = bank(free.pop(0))
+            passes = []
+            for w, x in plus[c]:
+                step = cols.stop - cols.start if w == "r" else QUARTER
+                passes.extend((w, x, slice(t0, t0 + step)) for t0 in range(cols.start, cols.stop, step))
+            for s, (w, x, part) in enumerate(passes):
+                product(sums[:, part], w, x, a, part, s == 0, s == len(passes) - 1)
+            finish(c, a, sums, [(cols, engine)])

@@ -55,8 +55,9 @@ def tile_mix_quat_relu_kernel(
             x_codes[c] = keep.tile([P, T], U32, name="x_codes_" + c, align_bytes=64)
             x_scales[c] = keep.tile([P, T], U8, name="x_scales_" + c, align_bytes=64)
             minus[c] = keep.tile([P, TILES, T], F32, name="minus_" + c)
-        for c in "jikr":
+        for c in "jkr":
             nc.vector.memset(w_scales[c][:].bitcast(U32), 0)
+        nc.gpsimd.memset(w_scales["i"][:].bitcast(U32), 0)
 
         def load_x(c, h):
             x_raw[c, h] = keep.tile([P, PACK, HALF], F32, name="x_raw_%s%d" % (c, h), align_bytes=64)
@@ -67,8 +68,9 @@ def tile_mix_quat_relu_kernel(
             nc.sync.dma_start(out=w_words[c][:].bitcast(I32), in_=words_hbm[c].bitcast(I32))
 
         def load_scales(c):
+            queue = nc.gpsimd if c == "i" else nc.sync
             for r in range(4):
-                nc.sync.dma_start(
+                queue.dma_start(
                     out=w_scales[c][r:P:32, :].bitcast(I32), in_=scales_hbm[c][r:16:4, :].bitcast(I32)
                 )
 
@@ -124,9 +126,9 @@ def tile_mix_quat_relu_kernel(
         halves = [slice(0, HALF), slice(HALF, T)]
         plus = {
             "r": [("r", "r")],
-            "i": [("j", "k"), ("i", "r"), ("r", "i")],
-            "j": [("k", "i"), ("j", "r"), ("r", "j")],
-            "k": [("i", "j"), ("k", "r"), ("r", "k")],
+            "i": [("j", "k"), ("r", "i"), ("i", "r")],
+            "j": [("k", "i"), ("r", "j"), ("j", "r")],
+            "k": [("i", "j"), ("r", "k"), ("k", "r")],
         }
 
         def lone_sum(c, w, x, h, b):
@@ -194,6 +196,14 @@ def tile_mix_quat_relu_kernel(
                 relu(engine, res[:], diff[:])
                 nc.sync.dma_start(out=out_hbm[c][a * P : (a + 1) * P, cols], in_=res[:])
 
+        def finish_in_halves(c, a, acc, engine):
+            res = keep.tile([P, T], F32, name="res_%s%d" % (c, a))
+            for cols in halves:
+                diff = keep.tile([P, HALF], F32, name="diff_%s%d_%d" % (c, a, cols.start))
+                nc.vector.tensor_tensor(out=diff[:], in0=acc[:, cols], in1=minus[c][:, a, cols], op=ALU.subtract)
+                relu(engine, res[:, cols], diff[:])
+            nc.sync.dma_start(out=out_hbm[c][a * P : (a + 1) * P, :], in_=res[:])
+
         free = [1, 4, 5, 6, 7]
         order = [(c, 0) for c in "jikr"] + [(c, a) for a in (1, 2, 3) for c in "rijk"]
         for n, (c, a) in enumerate(order[:-1]):
@@ -202,7 +212,9 @@ def tile_mix_quat_relu_kernel(
             sums, b = opened[c, a]
             for s, (w, x) in enumerate(plus[c][1:]):
                 product(sums[:], w, x, a, whole, False, s == 1)
-            if n >= len(order) - 2:
+            if n < 15:
+                finish_in_halves(c, a, sums, "gpsimd" if n < 2 else "scalar")
+            elif n >= len(order) - 2:
                 finish(c, a, sums, [(halves[0], "scalar"), (halves[1], "scalar")])
             else:
                 finish(c, a, sums, [(whole, "gpsimd" if n < 2 else "scalar")])

@@ -17,12 +17,28 @@ ALU = mybir.AluOpType
 
 P = 128
 PACK = 4
+TILES = N // P
 HALF = T // 2
 QUARTER = T // 4
-TILES = N // P
-BANKS = 8
-WARM_PASSES = 0
+RUN = 2
+QUADRANT = 32
 F32_MAX = 3.4028234663852886e38
+
+WHOLE = slice(0, T)
+HALVES = (slice(0, HALF), slice(HALF, T))
+WORD_SIZE = {"r": 4, "i": 2, "j": 2, "k": 2}
+WORD_VIEW = {"r": FP8X4, "i": FP4X4, "j": FP4X4, "k": FP4X4}
+
+ADDED = {
+    "r": (("r", "r"),),
+    "i": (("j", "k"), ("r", "i"), ("i", "r")),
+    "j": (("k", "i"), ("r", "j"), ("j", "r")),
+    "k": (("i", "j"), ("r", "k"), ("k", "r")),
+}
+SINGLE = {"i": ("k", "j"), "k": ("j", "i"), "j": ("i", "k")}
+
+TRIPLE_BANK = 4
+GPSIMD_RELUS = 2
 
 
 def tile_mix_quat_relu_kernel(
@@ -33,45 +49,41 @@ def tile_mix_quat_relu_kernel(
     nc = tc.nc
     x_hbm = {"r": xr, "i": xi, "j": xj, "k": xk}
     words_hbm = {
-        "r": wr_words[0].rearrange("p n t -> p (n t)"),
+        "r": wr_words[0].rearrange("p n e -> p (n e)"),
         "i": wi_words[0],
         "j": wj_words[0],
         "k": wk_words[0],
     }
     scales_hbm = {"r": wr_scales[0], "i": wi_scales[0], "j": wj_scales[0], "k": wk_scales[0]}
     out_hbm = {"r": out_0, "i": out_1, "j": out_2, "k": out_3}
-    word_size = {"r": 4, "i": 2, "j": 2, "k": 2}
-    word_view = {"r": FP8X4, "i": FP4X4, "j": FP4X4, "k": FP4X4}
 
     with ExitStack() as ctx:
         keep = ctx.enter_context(tc.tile_pool(name="keep", bufs=1))
         psum = ctx.enter_context(tc.psum_pool(name="psum", bufs=1))
         ctx.enter_context(tc.manual_schedule())
 
-        w_words, w_scales, x_raw, x_codes, x_scales, minus = {}, {}, {}, {}, {}, {}
-        for c in "jikr":
-            w_words[c] = keep.tile([P, N * word_size[c]], U8, name="w_words_" + c, align_bytes=64)
-            w_scales[c] = keep.tile([P, N], U8, name="w_scales_" + c, align_bytes=64)
-            x_codes[c] = keep.tile([P, T], U32, name="x_codes_" + c, align_bytes=64)
-            x_scales[c] = keep.tile([P, T], U8, name="x_scales_" + c, align_bytes=64)
-            minus[c] = keep.tile([P, TILES, T], F32, name="minus_" + c)
-        for c in "jkr":
-            nc.vector.memset(w_scales[c][:].bitcast(U32), 0)
-        nc.gpsimd.memset(w_scales["i"][:].bitcast(U32), 0)
+        w_words, w_scales, x_raw, x_codes, x_scales, subtracted = {}, {}, {}, {}, {}, {}
+        for part in "jikr":
+            w_words[part] = keep.tile([P, N * WORD_SIZE[part]], U8, name="w_words_" + part, align_bytes=64)
+            w_scales[part] = keep.tile([P, N], U8, name="w_scales_" + part, align_bytes=64)
+            x_codes[part] = keep.tile([P, T], U32, name="x_codes_" + part, align_bytes=64)
+            x_scales[part] = keep.tile([P, T], U8, name="x_scales_" + part, align_bytes=64)
+            subtracted[part] = keep.tile([P, TILES, T], F32, name="subtracted_" + part)
+            nc.vector.memset(w_scales[part][:].bitcast(U32), 0)
 
-        def load_x(c, h):
-            x_raw[c, h] = keep.tile([P, PACK, HALF], F32, name="x_raw_%s%d" % (c, h), align_bytes=64)
-            rows = x_hbm[c].rearrange("(p j) t -> p j t", j=PACK)
-            nc.sync.dma_start(out=x_raw[c, h][:], in_=rows[:, :, h * HALF : (h + 1) * HALF])
+        def load_x(part, half):
+            x_raw[part, half] = keep.tile([P, PACK, HALF], F32, name="x_raw_%s%d" % (part, half), align_bytes=64)
+            rows = x_hbm[part].rearrange("(p e) t -> p e t", e=PACK)
+            nc.sync.dma_start(out=x_raw[part, half][:], in_=rows[:, :, HALVES[half]])
 
-        def load_words(c):
-            nc.sync.dma_start(out=w_words[c][:].bitcast(I32), in_=words_hbm[c].bitcast(I32))
+        def load_words(part):
+            nc.sync.dma_start(out=w_words[part][:].bitcast(I32), in_=words_hbm[part].bitcast(I32))
 
-        def load_scales(c):
-            queue = nc.gpsimd if c == "i" else nc.sync
+        def load_scales(part):
             for r in range(4):
-                queue.dma_start(
-                    out=w_scales[c][r:P:32, :].bitcast(I32), in_=scales_hbm[c][r:16:4, :].bitcast(I32)
+                nc.sync.dma_start(
+                    out=w_scales[part][r:P:QUADRANT, :].bitcast(I32),
+                    in_=scales_hbm[part][r : K // QUADRANT : 4, :].bitcast(I32),
                 )
 
         load_x("i", 0)
@@ -91,30 +103,33 @@ def tile_mix_quat_relu_kernel(
         load_scales("r")
         load_words("r")
 
-        def quantize_half(c, h):
+        def quantize_half(part, half):
             grouped = []
             for q in range(2):
-                g = keep.tile([P, QUARTER, PACK], BF16, name="grouped_%s%d%d" % (c, h, q), align_bytes=64)
+                name = "grouped_%s%d%d" % (part, half, q)
+                quarter = keep.tile([P, QUARTER, PACK], BF16, name=name, align_bytes=64)
+                raw = x_raw[part, half][:, :, q * QUARTER : (q + 1) * QUARTER]
                 nc.vector.tensor_copy(
-                    out=g[:].rearrange("p (c i) t -> p c t i", i=4),
-                    in_=x_raw[c, h][:, :, q * QUARTER : (q + 1) * QUARTER].rearrange("p t (c i) -> p c t i", i=4),
+                    out=quarter[:].rearrange("p (c i) e -> p c e i", i=RUN),
+                    in_=raw.rearrange("p e (c i) -> p c e i", i=RUN),
                 )
-                grouped.append(g)
+                grouped.append(quarter)
             for q in range(2):
-                cols = slice(h * HALF + q * QUARTER, h * HALF + (q + 1) * QUARTER)
+                cols = slice(half * HALF + q * QUARTER, half * HALF + (q + 1) * QUARTER)
                 nc.vector.quantize_mx(
-                    out=x_codes[c][:, cols].bitcast(FP8X4),
-                    scales=x_scales[c][:, cols],
-                    in_=grouped[q][:].rearrange("p w t -> p (w t)"),
+                    out=x_codes[part][:, cols].bitcast(FP8X4),
+                    scales=x_scales[part][:, cols],
+                    in_=grouped[q][:].rearrange("p t e -> p (t e)"),
                 )
 
         def bank(b):
             return psum.tile([P, T], F32, name="bank%d" % b)
 
         def product(acc, w, x, a, cols, start, stop):
+            size = WORD_SIZE[w]
             nc.tensor.matmul_mx(
                 out=acc,
-                lhsT=w_words[w][:, a * P * word_size[w] : (a + 1) * P * word_size[w]].bitcast(word_view[w]),
+                lhsT=w_words[w][:, a * P * size : (a + 1) * P * size].bitcast(WORD_VIEW[w]),
                 lhsT_scale=w_scales[w][:, a * P : (a + 1) * P],
                 rhs=x_codes[x][:, cols].bitcast(FP8X4),
                 rhs_scale=x_scales[x][:, cols],
@@ -122,110 +137,94 @@ def tile_mix_quat_relu_kernel(
                 stop=stop,
             )
 
-        whole = slice(0, T)
-        halves = [slice(0, HALF), slice(HALF, T)]
-        plus = {
-            "r": [("r", "r")],
-            "i": [("j", "k"), ("r", "i"), ("i", "r")],
-            "j": [("k", "i"), ("r", "j"), ("j", "r")],
-            "k": [("i", "j"), ("r", "k"), ("k", "r")],
-        }
-
-        def lone_sum(c, w, x, h, b):
-            lone = bank(b)
-            u = b % 2
-            for v in range(2):
-                product(lone[:, halves[v]], w, x, 2 * u + v, halves[h], True, True)
+        def single_sums(x, half, pair, b):
+            part, w = SINGLE[x]
+            acc = bank(b)
+            for side in range(2):
+                product(acc[:, HALVES[side]], w, x, 2 * pair + side, HALVES[half], True, True)
             nc.scalar.activation(
-                out=minus[c][:, 2 * u : 2 * u + 2, halves[h]],
-                in_=lone[:].rearrange("p (v t) -> p v t", v=2),
+                out=subtracted[part][:, 2 * pair : 2 * pair + 2, HALVES[half]],
+                in_=acc[:].rearrange("p (side t) -> p side t", side=2),
                 func=ACT.Copy,
             )
 
-        def mr_half(x, h, tiles):
-            for a in tiles:
-                for q in range(2):
-                    part = slice(h * HALF + q * QUARTER, h * HALF + (q + 1) * QUARTER)
-                    product(m_r[a][:, part], x, x, a, part, False, h == 1 and q == 1)
+        added = {}
 
-        m_r = [bank(TILES + a) for a in range(TILES)]
-        opened = {}
+        def open_added(part, a, b):
+            added[part, a] = (bank(b), b)
+            w, x = ADDED[part][0]
+            product(added[part, a][0][:], w, x, a, WHOLE, True, len(ADDED[part]) == 1)
 
-        def open_sum(c, a, b):
-            opened[c, a] = (bank(b), b)
-            product(opened[c, a][0][:], *plus[c][0], a, whole, True, c == "r")
-
-        for x, lone_out, lone_w in (("i", "k", "j"), ("k", "j", "i"), ("j", "i", "k")):
-            quantize_half(x, 0)
-            lone_sum(lone_out, lone_w, x, 0, 0)
-            lone_sum(lone_out, lone_w, x, 0, 1)
-            quantize_half(x, 1)
-            if x != "j":
-                lone_sum(lone_out, lone_w, x, 1, 2)
-                lone_sum(lone_out, lone_w, x, 1, 3)
-                for a in range(TILES):
-                    product(m_r[a][:], x, x, a, whole, x == "i", False)
-        open_sum("j", 0, 2)
-        open_sum("i", 0, 3)
-        for step in (0, 4, 1, 2, 5, 3):
-            if step >= TILES:
-                lone_sum("i", "k", "j", 1, step - TILES)
+        def relu(engine, result, diff):
+            if engine == "scalar":
+                nc.scalar.activation(out=result, in_=diff, func=ACT.Relu)
+            elif engine == "vector":
+                nc.vector.tensor_scalar_max(out=result, in0=diff, scalar1=0.0)
             else:
-                product(m_r[step][:], "j", "j", step, whole, False, True)
+                nc.gpsimd.tensor_scalar(
+                    out=result, in0=diff, scalar1=F32_MAX, scalar2=0.0, op0=ALU.min, op1=ALU.max
+                )
+
+        def finish(part, a, acc, pieces, engine):
+            first, last = pieces[0].start, pieces[-1].stop
+            result = keep.tile([P, last - first], F32, name="result_%s%d_%d" % (part, a, first))
+            for cols in pieces:
+                diff = keep.tile([P, cols.stop - cols.start], F32, name="diff_%s%d_%d" % (part, a, cols.start))
+                nc.vector.tensor_tensor(
+                    out=diff[:], in0=acc[:, cols], in1=subtracted[part][:, a, cols], op=ALU.subtract
+                )
+                relu(engine, result[:, cols.start - first : cols.stop - first], diff[:])
+            nc.sync.dma_start(out=out_hbm[part][a * P : (a + 1) * P, first:last], in_=result[:])
+
+        triple = [bank(TRIPLE_BANK + a) for a in range(TILES)]
+        for x in "ik":
+            for half in range(2):
+                quantize_half(x, half)
+                for pair in range(2):
+                    single_sums(x, half, pair, 2 * half + pair)
+            for a in range(TILES):
+                product(triple[a][:], x, x, a, WHOLE, x == "i", False)
+
+        quantize_half("j", 0)
+        for pair in range(2):
+            single_sums("j", 0, pair, pair)
+        quantize_half("j", 1)
+        open_added("j", 0, 2)
+        open_added("i", 0, 3)
+        for pair in range(2):
+            product(triple[2 * pair][:], "j", "j", 2 * pair, WHOLE, False, True)
+            single_sums("j", 1, pair, pair)
+            product(triple[2 * pair + 1][:], "j", "j", 2 * pair + 1, WHOLE, False, True)
         for a in range(TILES):
-            nc.scalar.activation(out=minus["r"][:, a, :], in_=m_r[a][:], func=ACT.Copy)
+            nc.scalar.activation(out=subtracted["r"][:, a, :], in_=triple[a][:], func=ACT.Copy)
+
         quantize_half("r", 0)
         quantize_half("r", 1)
-        open_sum("k", 0, 0)
-        def relu(engine, res, diff):
-            if engine == "scalar":
-                nc.scalar.activation(out=res, in_=diff, func=ACT.Relu)
-            elif engine == "vector":
-                nc.vector.tensor_scalar_max(out=res, in0=diff, scalar1=0.0)
+        open_added("k", 0, 0)
+
+        free = [1] + [TRIPLE_BANK + a for a in range(TILES)]
+        order = [(part, 0) for part in "jikr"] + [(part, a) for a in range(1, TILES) for part in "rijk"]
+        for n, (part, a) in enumerate(order[:-1]):
+            if (part, a) not in added:
+                open_added(part, a, free.pop(0))
+            acc, b = added[part, a]
+            for w, x in ADDED[part][1:]:
+                product(acc[:], w, x, a, WHOLE, False, x == "r")
+            if n < GPSIMD_RELUS:
+                finish(part, a, acc, HALVES, "gpsimd")
+            elif n == len(order) - 2:
+                finish(part, a, acc, HALVES, "scalar")
             else:
-                nc.gpsimd.tensor_scalar(out=res, in0=diff, scalar1=F32_MAX, scalar2=0.0, op0=ALU.min, op1=ALU.max)
-
-        def finish(c, a, acc, pieces):
-            diffs = []
-            for cols, engine in pieces:
-                diff = keep.tile([P, cols.stop - cols.start], F32, name="diff_%s%d_%d" % (c, a, cols.start))
-                nc.vector.tensor_tensor(out=diff[:], in0=acc[:, cols], in1=minus[c][:, a, cols], op=ALU.subtract)
-                diffs.append(diff)
-            for diff, (cols, engine) in zip(diffs, pieces):
-                res = keep.tile([P, cols.stop - cols.start], F32, name="res_%s%d_%d" % (c, a, cols.start))
-                relu(engine, res[:], diff[:])
-                nc.sync.dma_start(out=out_hbm[c][a * P : (a + 1) * P, cols], in_=res[:])
-
-        def finish_in_halves(c, a, acc, engine):
-            res = keep.tile([P, T], F32, name="res_%s%d" % (c, a))
-            for cols in halves:
-                diff = keep.tile([P, HALF], F32, name="diff_%s%d_%d" % (c, a, cols.start))
-                nc.vector.tensor_tensor(out=diff[:], in0=acc[:, cols], in1=minus[c][:, a, cols], op=ALU.subtract)
-                relu(engine, res[:, cols], diff[:])
-            nc.sync.dma_start(out=out_hbm[c][a * P : (a + 1) * P, :], in_=res[:])
-
-        free = [1, 4, 5, 6, 7]
-        order = [(c, 0) for c in "jikr"] + [(c, a) for a in (1, 2, 3) for c in "rijk"]
-        for n, (c, a) in enumerate(order[:-1]):
-            if (c, a) not in opened:
-                open_sum(c, a, free.pop(0))
-            sums, b = opened[c, a]
-            for s, (w, x) in enumerate(plus[c][1:]):
-                product(sums[:], w, x, a, whole, False, s == 1)
-            if n < 15:
-                finish_in_halves(c, a, sums, "gpsimd" if n < 2 else "scalar")
-            elif n >= len(order) - 2:
-                finish(c, a, sums, [(halves[0], "scalar"), (halves[1], "scalar")])
-            else:
-                finish(c, a, sums, [(whole, "gpsimd" if n < 2 else "scalar")])
+                finish(part, a, acc, (WHOLE,), "scalar")
             free.append(b)
-        c, a = order[-1]
-        for cols, engine in ((halves[0], "scalar"), (halves[1], "vector")):
-            sums = bank(free.pop(0))
+
+        part, a = order[-1]
+        for cols, engine in zip(HALVES, ("scalar", "vector")):
+            acc = bank(free.pop(0))
             passes = []
-            for w, x in plus[c]:
-                step = cols.stop - cols.start if w == "r" else QUARTER
-                passes.extend((w, x, slice(t0, t0 + step)) for t0 in range(cols.start, cols.stop, step))
-            for s, (w, x, part) in enumerate(passes):
-                product(sums[:, part], w, x, a, part, s == 0, s == len(passes) - 1)
-            finish(c, a, sums, [(cols, engine)])
+            for w, x in ADDED[part]:
+                width = HALF if w == "r" else QUARTER
+                passes.extend((w, x, slice(t0, t0 + width)) for t0 in range(cols.start, cols.stop, width))
+            for s, (w, x, span) in enumerate(passes):
+                product(acc[:, span], w, x, a, span, s == 0, s == len(passes) - 1)
+            finish(part, a, acc, (cols,), engine)

from contextlib import ExitStack

import concourse.mybir as mybir

K, N, T = 512, 512, 512
FLOPS = 16 * 2 * K * N * T

F32 = mybir.dt.float32
BF16 = mybir.dt.bfloat16
I32 = mybir.dt.int32
U32 = mybir.dt.uint32
U8 = mybir.dt.uint8
FP8X4 = mybir.dt.float8_e4m3fn_x4
FP4X4 = mybir.dt.float4_e2m1fn_x4
ACT = mybir.ActivationFunctionType
ALU = mybir.AluOpType

P = 128
PACK = 4
TILES = N // P
HALF = T // 2
QUARTER = T // 4
RUN = 2
QUADRANT = 32
F32_MAX = 3.4028234663852886e38

WHOLE = slice(0, T)
HALVES = (slice(0, HALF), slice(HALF, T))
WORD_SIZE = {"r": 4, "i": 2, "j": 2, "k": 2}
WORD_VIEW = {"r": FP8X4, "i": FP4X4, "j": FP4X4, "k": FP4X4}

ADDED = {
    "r": (("r", "r"),),
    "i": (("j", "k"), ("r", "i"), ("i", "r")),
    "j": (("k", "i"), ("r", "j"), ("j", "r")),
    "k": (("i", "j"), ("r", "k"), ("k", "r")),
}
SINGLE = {"i": ("k", "j"), "k": ("j", "i"), "j": ("i", "k")}

TRIPLE_BANK = 4
GPSIMD_RELUS = 2


def tile_mix_quat_relu_kernel(
    tc, xr, xi, xj, xk,
    wr_words, wr_scales, wi_words, wi_scales, wj_words, wj_scales, wk_words, wk_scales,
    out_0, out_1, out_2, out_3,
):
    nc = tc.nc
    x_hbm = {"r": xr, "i": xi, "j": xj, "k": xk}
    words_hbm = {
        "r": wr_words[0].rearrange("p n e -> p (n e)"),
        "i": wi_words[0],
        "j": wj_words[0],
        "k": wk_words[0],
    }
    scales_hbm = {"r": wr_scales[0], "i": wi_scales[0], "j": wj_scales[0], "k": wk_scales[0]}
    out_hbm = {"r": out_0, "i": out_1, "j": out_2, "k": out_3}

    with ExitStack() as ctx:
        keep = ctx.enter_context(tc.tile_pool(name="keep", bufs=1))
        psum = ctx.enter_context(tc.psum_pool(name="psum", bufs=1))
        ctx.enter_context(tc.manual_schedule())

        w_words, w_scales, x_raw, x_codes, x_scales, subtracted = {}, {}, {}, {}, {}, {}
        for part in "jikr":
            w_words[part] = keep.tile([P, N * WORD_SIZE[part]], U8, name="w_words_" + part, align_bytes=64)
            w_scales[part] = keep.tile([P, N], U8, name="w_scales_" + part, align_bytes=64)
            x_codes[part] = keep.tile([P, T], U32, name="x_codes_" + part, align_bytes=64)
            x_scales[part] = keep.tile([P, T], U8, name="x_scales_" + part, align_bytes=64)
            subtracted[part] = keep.tile([P, TILES, T], F32, name="subtracted_" + part)
            nc.vector.memset(w_scales[part][:].bitcast(U32), 0)

        def load_x(part, half):
            x_raw[part, half] = keep.tile([P, PACK, HALF], F32, name="x_raw_%s%d" % (part, half), align_bytes=64)
            rows = x_hbm[part].rearrange("(p e) t -> p e t", e=PACK)
            nc.sync.dma_start(out=x_raw[part, half][:], in_=rows[:, :, HALVES[half]])

        def load_words(part):
            nc.sync.dma_start(out=w_words[part][:].bitcast(I32), in_=words_hbm[part].bitcast(I32))

        def load_scales(part):
            for r in range(4):
                nc.sync.dma_start(
                    out=w_scales[part][r:P:QUADRANT, :].bitcast(I32),
                    in_=scales_hbm[part][r : K // QUADRANT : 4, :].bitcast(I32),
                )

        load_x("i", 0)
        load_words("j")
        load_scales("j")
        load_x("i", 1)
        load_x("k", 0)
        load_words("i")
        load_scales("i")
        load_x("k", 1)
        load_x("j", 0)
        load_words("k")
        load_scales("k")
        load_x("j", 1)
        load_x("r", 0)
        load_x("r", 1)
        load_scales("r")
        load_words("r")

        def quantize_half(part, half):
            grouped = []
            for q in range(2):
                name = "grouped_%s%d%d" % (part, half, q)
                quarter = keep.tile([P, QUARTER, PACK], BF16, name=name, align_bytes=64)
                raw = x_raw[part, half][:, :, q * QUARTER : (q + 1) * QUARTER]
                nc.vector.tensor_copy(
                    out=quarter[:].rearrange("p (c i) e -> p c e i", i=RUN),
                    in_=raw.rearrange("p e (c i) -> p c e i", i=RUN),
                )
                grouped.append(quarter)
            for q in range(2):
                cols = slice(half * HALF + q * QUARTER, half * HALF + (q + 1) * QUARTER)
                nc.vector.quantize_mx(
                    out=x_codes[part][:, cols].bitcast(FP8X4),
                    scales=x_scales[part][:, cols],
                    in_=grouped[q][:].rearrange("p t e -> p (t e)"),
                )

        def bank(b):
            return psum.tile([P, T], F32, name="bank%d" % b)

        def product(acc, w, x, a, cols, start, stop):
            size = WORD_SIZE[w]
            nc.tensor.matmul_mx(
                out=acc,
                lhsT=w_words[w][:, a * P * size : (a + 1) * P * size].bitcast(WORD_VIEW[w]),
                lhsT_scale=w_scales[w][:, a * P : (a + 1) * P],
                rhs=x_codes[x][:, cols].bitcast(FP8X4),
                rhs_scale=x_scales[x][:, cols],
                start=start,
                stop=stop,
            )

        def single_sums(x, half, pair, b):
            part, w = SINGLE[x]
            acc = bank(b)
            for side in range(2):
                product(acc[:, HALVES[side]], w, x, 2 * pair + side, HALVES[half], True, True)
            nc.scalar.activation(
                out=subtracted[part][:, 2 * pair : 2 * pair + 2, HALVES[half]],
                in_=acc[:].rearrange("p (side t) -> p side t", side=2),
                func=ACT.Copy,
            )

        added = {}

        def open_added(part, a, b):
            added[part, a] = (bank(b), b)
            w, x = ADDED[part][0]
            product(added[part, a][0][:], w, x, a, WHOLE, True, len(ADDED[part]) == 1)

        def relu(engine, result, diff):
            if engine == "scalar":
                nc.scalar.activation(out=result, in_=diff, func=ACT.Relu)
            elif engine == "vector":
                nc.vector.tensor_scalar_max(out=result, in0=diff, scalar1=0.0)
            else:
                nc.gpsimd.tensor_scalar(
                    out=result, in0=diff, scalar1=F32_MAX, scalar2=0.0, op0=ALU.min, op1=ALU.max
                )

        def finish(part, a, acc, pieces, engine):
            first, last = pieces[0].start, pieces[-1].stop
            result = keep.tile([P, last - first], F32, name="result_%s%d_%d" % (part, a, first))
            for cols in pieces:
                diff = keep.tile([P, cols.stop - cols.start], F32, name="diff_%s%d_%d" % (part, a, cols.start))
                nc.vector.tensor_tensor(
                    out=diff[:], in0=acc[:, cols], in1=subtracted[part][:, a, cols], op=ALU.subtract
                )
                relu(engine, result[:, cols.start - first : cols.stop - first], diff[:])
            nc.sync.dma_start(out=out_hbm[part][a * P : (a + 1) * P, first:last], in_=result[:])

        triple = [bank(TRIPLE_BANK + a) for a in range(TILES)]
        for x in "ik":
            for half in range(2):
                quantize_half(x, half)
                for pair in range(2):
                    single_sums(x, half, pair, 2 * half + pair)
            for a in range(TILES):
                product(triple[a][:], x, x, a, WHOLE, x == "i", False)

        quantize_half("j", 0)
        for pair in range(2):
            single_sums("j", 0, pair, pair)
        quantize_half("j", 1)
        open_added("j", 0, 2)
        open_added("i", 0, 3)
        for pair in range(2):
            product(triple[2 * pair][:], "j", "j", 2 * pair, WHOLE, False, True)
            single_sums("j", 1, pair, pair)
            product(triple[2 * pair + 1][:], "j", "j", 2 * pair + 1, WHOLE, False, True)
        for a in range(TILES):
            nc.scalar.activation(out=subtracted["r"][:, a, :], in_=triple[a][:], func=ACT.Copy)

        quantize_half("r", 0)
        quantize_half("r", 1)
        open_added("k", 0, 0)

        free = [1] + [TRIPLE_BANK + a for a in range(TILES)]
        order = [(part, 0) for part in "jikr"] + [(part, a) for a in range(1, TILES) for part in "rijk"]
        for n, (part, a) in enumerate(order[:-1]):
            if (part, a) not in added:
                open_added(part, a, free.pop(0))
            acc, b = added[part, a]
            for w, x in ADDED[part][1:]:
                product(acc[:], w, x, a, WHOLE, False, x == "r")
            if n < GPSIMD_RELUS:
                finish(part, a, acc, HALVES, "gpsimd")
            elif n == len(order) - 2:
                finish(part, a, acc, HALVES, "scalar")
            else:
                finish(part, a, acc, (WHOLE,), "scalar")
            free.append(b)

        part, a = order[-1]
        for cols, engine in zip(HALVES, ("scalar", "vector")):
            acc = bank(free.pop(0))
            passes = []
            for w, x in ADDED[part]:
                width = HALF if w == "r" else QUARTER
                passes.extend((w, x, slice(t0, t0 + width)) for t0 in range(cols.start, cols.stop, width))
            for s, (w, x, span) in enumerate(passes):
                product(acc[:, span], w, x, a, span, s == 0, s == len(passes) - 1)
            finish(part, a, acc, (cols,), engine)
